import numpy as np, ml_dtypes
CORES = [5,29,101,125,133,157,229,253]
N = 8
import mx_ref
NC, G = 512, 4
EPS = 0.001
BF = ml_dtypes.bfloat16
def cut(t, i, w=512):
    return t[:, w * i:w * i + w]
def tile(rs):
    return np.stack(rs, axis=2).reshape(128, -1).astype(BF)
def layer(w, X):
    out = []
    for i in range(G):
        for t in range(len(X)):
            p = mx_ref.matmul(mx_ref.quantize(cut(w, len(X) * i + t)), X[t])
            z = p if t == 0 else z + p
        out.append(z)
    return out
def setup_inputs(rng):
    def f(*shape):
        return mx_ref.flush((rng.standard_normal(shape, dtype=np.float32) * np.exp2(rng.integers(-2, 3, shape[:-1] + (1,)))).astype(BF))
    return {"x": f(N, 128, 4 * NC), "w1": f(N, 128, G * 512), "w2": f(N, 128, 2 * 512)}
def setup_inputs_blocks(rng):
    d = setup_inputs(rng)
    for k in ("x", "w1", "w2"): d[k] = mx_ref.spread(d[k], rng, 4)
    return d
def setup_inputs_wide(rng):
    d = setup_inputs(rng)
    for k in ("x", "w1", "w2"): d[k] = mx_ref.flush((d[k].astype(np.float32) * np.exp2(rng.integers(-6, 7, (N, 1, 1))).astype(np.float32)).astype(BF))
    return d
def setup_inputs_cols(rng):
    d = setup_inputs(rng); v = d["x"].astype(np.float32).reshape(N, 128, -1, 4)
    d["x"] = mx_ref.flush((v * np.exp2(rng.integers(-6, 7, (N, 1, v.shape[2], 1))).astype(np.float32)).reshape(d["x"].shape).astype(BF))
    return d
def setup_inputs_faint(rng):
    d = setup_inputs(rng); d["x"] = mx_ref.flush((d["x"].astype(np.float32) * np.float32(2.0 ** -12)).astype(BF))
    return d
def reference(x, w1, w2, own=None):
    h = np.zeros((N, 128, 4 * NC), BF)
    for r in range(N):
        Z = layer(w1[r], [mx_ref.quantize(x[r])]); R = Z
        ms = sum((v.astype(np.float64) ** 2).sum(axis=0) for v in R) / 512
        s = (1 / np.sqrt(ms + EPS)).astype(np.float32)
        h[r] = tile([v * s for v in R])
    use = h if own is None else own["h"]
    H = [mx_ref.quantize(use[j]) for j in range(N)]
    y = np.zeros((N, 128, NC), np.float32)
    for r in range(N):
        y[r] = mx_ref.matmul(mx_ref.quantize(cut(w2[r], 0)), H[r]) + mx_ref.matmul(mx_ref.quantize(cut(w2[r], 1)), H[(r + 1) % N])
    return {"h": h, "y": y}

@@ -1,0 +1,248 @@
+from concourse.bass import DstId, RemoteDMATransfer
+from concourse.mybir import dt, AluOpType, ActivationFunctionType
+
+NS = 4
+SW = 128
+EPS = 0.001
+ROWS = 512
+ROUTE = (0, 1, 0, 1, 0)
+
+SCRATCH = {
+    "xt": ("sbuf", [128, 2048], "bfloat16"),
+    "w1t": ("sbuf", [128, 2048], "bfloat16"),
+    "w2t": ("sbuf", [128, 1024], "bfloat16"),
+    "xq": ("sbuf", [128, 512], "float8_e4m3fn_x4"),
+    "xs": ("sbuf", [128, 512], "uint8"),
+    "w1q": ("sbuf", [128, 512], "float8_e4m3fn_x4"),
+    "w1s": ("sbuf", [128, 512], "uint8"),
+    "w2q": ("sbuf", [128, 256], "float8_e4m3fn_x4"),
+    "w2s": ("sbuf", [128, 256], "uint8"),
+    "ident": ("sbuf", [128, 128], "bfloat16"),
+    "sqr": ("sbuf", [128, 512], "float32"),
+    "st": ("sbuf", [128, 24], "float32"),
+    "rt": ("sbuf", [128, 2048], "bfloat16"),
+    "ht": ("sbuf", [128, 2048], "bfloat16"),
+    "hq": ("sbuf", [128, 512], "float8_e4m3fn_x4"),
+    "hs": ("sbuf", [128, 512], "uint8"),
+    "rq": ("sbuf", [128, 512], "float8_e4m3fn_x4"),
+    "rs": ("sbuf", [128, 512], "uint8"),
+    "yt": ("sbuf", [128, 512], "float32"),
+    "zp": ("psum", [128, 2048], "float32"),
+    "ze": ("psum", [128, 512], "float32"),
+    "yp": ("psum", [128, 1024], "float32"),
+}
+STAGES = ("qx", "mx", "sq", "ro", "vv", "rc", "nt", "nu", "sc", "tr", "cp", "qh")
+SEMAPHORES = (["%s%d" % (s, c) for s in STAGES for c in range(NS)]
+              + ["in%d" % i for i in range(NS + 1)]
+              + ["lx0", "lx1", "lw1", "lw2", "one", "idn", "qw1", "qw2", "te", "ya", "yb", "cy",
+                 "left", "sent", "arr", "sth", "sty"])
+
+
+def _bits(mask):
+    return [i for i in range(mask.bit_length()) if (mask >> i) & 1]
+
+
+def _mask(bits):
+    m = 0
+    for i in bits:
+        m |= 1 << i
+    return m
+
+
+def _plan(T, topo):
+    cores = list(T.cores)
+    n = len(cores)
+    world = range(topo.CORES_PER_HOST * (1 + max(topo.host(c) for c in cores)))
+    plan = []
+    for s in range(n):
+        src, dst = cores[s], cores[(s - 1) % n]
+        cand = [c for c in world
+                if topo.host(c) == topo.host(src) and topo.chip(c) == topo.chip(src) and c not in cores
+                and topo.may_write(src, c) and topo.may_write(c, dst)]
+        near = [c for c in cand if topo.die(c) == topo.die(src)]
+        far = [c for c in cand if topo.die(c) != topo.die(src)]
+        first = (near + far)[0]
+        second = [c for c in far + near if c != first][0]
+        plan.append((src, dst, (first, second)))
+    return plan
+
+
+def _piece(q, s, i):
+    if i < NS:
+        return q[:, SW * i:SW * i + SW].bitcast(dt.uint8)
+    return s[:]
+
+
+def _helper(g, core, T, topo, src, dst, which):
+    rid, pid = topo.addr(dst, core)
+    out_mask = topo.mask(core, dst)
+    landed = len(_bits(topo.mask(src, core))) // 2
+    mine = [i for i in range(NS + 1) if ROUTE[i] == which]
+    for i in mine:
+        g.wait_ge(T.sem["in%d" % i], landed)
+        g.remote_dma(out_ap=_piece(T.rq, T.rs, i), in_ap=_piece(T.rq, T.rs, i), remote_sem=T.sem.arr,
+                     local_sem=T.sem.sent, pid=pid, routing_id=rid, dma_engine_mask=out_mask)
+    g.wait_ge(T.sem.sent, len(_bits(out_mask)) * len(mine))
+
+
+def _rank(g, core, T, topo, helpers, arrivals):
+    S = T.sem
+    AF, OP = ActivationFunctionType, AluOpType
+    ve, te, sc, sy = g.vector, g.tensor, g.scalar, g.sync
+
+    def col(k, c):
+        return T.st[:, NS * k + c:NS * k + c + 1]
+
+    def sl(t, c, w):
+        return t[:, w * c:w * c + w]
+
+    sy.dma_start(T.xt[:, 0:4 * SW], T.x[:, 0:4 * SW]).then_inc(S.lx0, 16)
+    sc.dma_start(T.w1t[:], T.w1[:]).then_inc(S.lw1, 16)
+    sy.dma_start(T.xt[:, 4 * SW:], T.x[:, 4 * SW:]).then_inc(S.lx1, 16)
+    sc.dma_start(T.w2t[:], T.w2[:]).then_inc(S.lw2, 16)
+
+    ve.memset(T.ident[:], 1.0).then_inc(S.one, 1)
+    g.wait_ge(S.one, 1)
+    g.affine_select(T.ident[:], T.ident[:], [[-1, 128]], OP.is_equal, 0.0, 0, 1).then_inc(S.idn, 1)
+
+    def pack_x(c):
+        ve.quantize_mx(sl(T.xq, c, SW), sl(T.xs, c, SW), sl(T.xt, c, 4 * SW)).then_inc(S["qx%d" % c], 1)
+
+    def norm(c):
+        ve.wait_ge(S["sq%d" % c], 1)
+        ve.tensor_scalar(col(2, c), col(0, c), 1.0 / ROWS, EPS, OP.mult, OP.add).then_inc(S["vv%d" % c], 1)
+        ve.wait_ge(S["ro%d" % c], 1)
+        ve.reciprocal(col(3, c), col(1, c)).then_inc(S["rc%d" % c], 1)
+        ve.wait_ge(S["vv%d" % c], 1)
+        ve.wait_ge(S["rc%d" % c], 1)
+        ve.tensor_scalar(col(4, c), col(3, c), col(3, c), col(2, c), OP.mult, OP.mult).then_inc(S["nt%d" % c], 1)
+        ve.wait_ge(S["nt%d" % c], 1)
+        ve.tensor_scalar(col(5, c), col(4, c), -0.5, 1.5, OP.mult, OP.add).then_inc(S["nu%d" % c], 1)
+        ve.wait_ge(S["nu%d" % c], 1)
+        ve.wait_ge(S["mx%d" % c], 1)
+        ve.tensor_scalar(sl(T.rt, c, 4 * SW), sl(T.zp, c, 4 * SW), col(3, c), col(5, c),
+                         OP.mult, OP.mult).then_inc(S["sc%d" % c], 1)
+
+    def pack_h(c):
+        ve.wait_ge(S["cp%d" % c], 4)
+        ve.quantize_mx(sl(T.hq, c, SW), sl(T.hs, c, SW), sl(T.ht, c, 4 * SW)).then_inc(S["qh%d" % c], 1)
+
+    def h_cols(c, b):
+        return T.ht[:, 4 * SW * c + b:4 * SW * (c + 1):4]
+
+    last = NS - 1
+    ve.wait_ge(S.lx0, 16)
+    pack_x(0)
+    ve.wait_ge(S.lw1, 16)
+    ve.quantize_mx(T.w1q[:], T.w1s[:], T.w1t[:]).then_inc(S.qw1, 1)
+    ve.wait_ge(S.lx1, 16)
+    for c in range(1, NS):
+        pack_x(c)
+    norm(0)
+    for c in range(1, NS):
+        norm(c)
+        pack_h(c - 1)
+    ve.wait_ge(S["tr%d" % last], 2)
+    for b in (0, 1):
+        ve.tensor_copy(h_cols(last, b), T.zp[:, 4 * SW * last + SW * b:4 * SW * last + SW * b + SW]).then_inc(S["cp%d" % last], 1)
+    pack_h(last)
+    ve.wait_ge(S.lw2, 16)
+    ve.quantize_mx(T.w2q[:], T.w2s[:], T.w2t[:]).then_inc(S.qw2, 1)
+    ve.wait_ge(S.ya, 1)
+    ve.tensor_copy(T.yt[:, 0:256], T.yp[:, 0:256]).then_inc(S.cy, 1)
+
+    def stats(c):
+        sc.wait_ge(S["mx%d" % c], 1)
+        sc.activation(T.sqr[:], sl(T.zp, c, 4 * SW), AF.Square, accum_out=col(0, c)).then_inc(S["sq%d" % c], 1)
+        sc.wait_ge(S["sq%d" % c], 1)
+        sc.activation(col(1, c), col(0, c), AF.Sqrt, bias=EPS, scale=1.0 / ROWS).then_inc(S["ro%d" % c], 1)
+
+    def back(c):
+        sc.wait_ge(S["tr%d" % c], 4)
+        for b in range(4):
+            sc.activation(h_cols(c, b), T.zp[:, 4 * SW * c + SW * b:4 * SW * c + SW * b + SW], AF.Copy).then_inc(S["cp%d" % c], 1)
+
+    stats(0)
+    stats(1)
+    stats(2)
+    back(0)
+    stats(3)
+    back(1)
+    back(2)
+    sc.wait_ge(S.te, 2)
+    for b in (2, 3):
+        sc.activation(h_cols(last, b), T.ze[:, SW * (b - 2):SW * (b - 1)], AF.Copy).then_inc(S["cp%d" % last], 1)
+    sc.wait_ge(S.yb, 1)
+    sc.activation(T.yt[:, 256:512], T.yp[:, 512:768], AF.Copy).then_inc(S.cy, 1)
+
+    te.wait_ge(S.qw1, 1)
+    for c in range(NS):
+        te.wait_ge(S["qx%d" % c], 1)
+        te.matmul_mx(sl(T.zp, c, 4 * SW), sl(T.xq, c, SW), sl(T.xs, c, SW), T.w1q[:], T.w1s[:],
+                     True, True).then_inc(S["mx%d" % c], 1)
+    te.wait_ge(S.idn, 1)
+    for c in range(NS):
+        te.wait_ge(S["sc%d" % c], 1)
+        for b in range(4):
+            turned = T.rt[:, 4 * SW * c + SW * b:4 * SW * c + SW * b + SW]
+            if c == last and b >= 2:
+                te.matmul(T.ze[:, SW * (b - 2):SW * (b - 1)], turned, T.ident[:], True, True).then_inc(S.te, 1)
+            else:
+                te.matmul(T.zp[:, 4 * SW * c + SW * b:4 * SW * c + SW * b + SW], turned, T.ident[:],
+                          True, True).then_inc(S["tr%d" % c], 1)
+    te.wait_ge(S.qw2, 1)
+    for c in range(NS):
+        te.wait_ge(S["qh%d" % c], 1)
+    for k in range(2):
+        te.matmul_mx(T.yp[:, 512 * k:512 * k + 256], T.w2q[:, 0:128], T.w2s[:, 0:128],
+                     T.hq[:, 256 * k:256 * k + 256], T.hs[:, 256 * k:256 * k + 256], True, False)
+    te.wait_ge(S.arr, arrivals)
+    for k in range(2):
+        te.matmul_mx(T.yp[:, 512 * k:512 * k + 256], T.w2q[:, 128:256], T.w2s[:, 128:256],
+                     T.rq[:, 256 * k:256 * k + 256], T.rs[:, 256 * k:256 * k + 256], False, True).then_inc((S.ya, S.yb)[k], 1)
+
+    where, engines = [], []
+    for k in range(2):
+        where.append(topo.addr(helpers[k], core))
+        bits = _bits(topo.mask(core, helpers[k]))
+        half = len(bits) // 2
+        engines.append(_mask(bits[half * k:half * k + half]))
+    left = 0
+    for i in range(NS - 1):
+        k = ROUTE[i]
+        g.wait_ge(S["qh%d" % i], 1)
+        g.remote_dma(out_ap=_piece(T.rq, T.rs, i), in_ap=_piece(T.hq, T.hs, i), remote_sem=S["in%d" % i],
+                     local_sem=S.left, pid=where[k][1], routing_id=where[k][0], dma_engine_mask=engines[k])
+        left += len(_bits(engines[k]))
+    g.wait_ge(S["qh%d" % last], 1)
+    both = []
+    for i in (NS - 1, NS):
+        k = ROUTE[i]
+        both.append(RemoteDMATransfer(dst_ids=[DstId(rid=where[k][0], pnc=where[k][1])], dma_engine_mask=engines[k],
+                                      remote_sem=S["in%d" % i], src=_piece(T.hq, T.hs, i), dst=_piece(T.rq, T.rs, i)))
+        left += len(_bits(engines[k]))
+    g.remote_dma_fused(both, local_sem=S.left)
+
+    for c in range(NS):
+        sy.wait_ge(S["cp%d" % c], 4)
+    sy.wait_ge(S.left, left)
+    sy.dma_start(T.h[:], T.ht[:]).then_inc(S.sth, 16)
+    sy.wait_ge(S.cy, 2)
+    sy.dma_start(T.y[:], T.yt[:]).then_inc(S.sty, 16)
+    sy.wait_ge(S.sth, 16)
+    sy.wait_ge(S.sty, 16)
+
+
+def rank_program(g, core, T, topo):
+    plan = _plan(T, topo)
+    n = len(plan)
+    rank = T.rank_of(core)
+    if rank is not None:
+        src, dst, helpers = plan[(rank + 1) % n]
+        arrivals = sum(len(_bits(topo.mask(helpers[ROUTE[i]], dst))) for i in range(NS + 1))
+        _rank(g, core, T, topo, plan[rank][2], arrivals)
+        return
+    for src, dst, helpers in plan:
+        for k in range(2):
+            if helpers[k] == core:
+                _helper(g, core, T, topo, src, dst, k)

@@ -2,10 +2,11 @@ from concourse.bass import DstId, RemoteDMATransfer
 from concourse.mybir import dt, AluOpType, ActivationFunctionType
 
 NS = 4
+NB = 4
 SW = 128
+BANK = 512
 EPS = 0.001
 ROWS = 512
-ROUTE = (0, 1, 0, 1, 0)
 
 SCRATCH = {
     "xt": ("sbuf", [128, 2048], "bfloat16"),
@@ -19,7 +20,7 @@ SCRATCH = {
     "w2s": ("sbuf", [128, 256], "uint8"),
     "ident": ("sbuf", [128, 128], "bfloat16"),
     "sqr": ("sbuf", [128, 512], "float32"),
-    "st": ("sbuf", [128, 24], "float32"),
+    "st": ("sbuf", [128, 32], "float32"),
     "rt": ("sbuf", [128, 2048], "bfloat16"),
     "ht": ("sbuf", [128, 2048], "bfloat16"),
     "hq": ("sbuf", [128, 512], "float8_e4m3fn_x4"),
@@ -27,15 +28,14 @@ SCRATCH = {
     "rq": ("sbuf", [128, 512], "float8_e4m3fn_x4"),
     "rs": ("sbuf", [128, 512], "uint8"),
     "yt": ("sbuf", [128, 512], "float32"),
-    "zp": ("psum", [128, 2048], "float32"),
-    "ze": ("psum", [128, 512], "float32"),
-    "yp": ("psum", [128, 1024], "float32"),
+    "pe": ("psum", [128, 2048], "float32"),
+    "zp": ("psum", [128, 1536], "float32"),
 }
-STAGES = ("qx", "mx", "sq", "ro", "vv", "rc", "nt", "nu", "sc", "tr", "cp", "qh")
+STAGES = ("qx", "mx", "sq", "ro", "vv", "rc", "nt", "nu", "sc", "tr", "cp", "qh", "ic", "ip", "arr", "ym", "cy")
+BLOCKS = ("wq", "ma", "sa", "ta", "sz", "tz")
 SEMAPHORES = (["%s%d" % (s, c) for s in STAGES for c in range(NS)]
-              + ["in%d" % i for i in range(NS + 1)]
-              + ["lx0", "lx1", "lw1", "lw2", "one", "idn", "qw1", "qw2", "te", "ya", "yb", "cy",
-                 "left", "sent", "arr", "sth", "sty"])
+              + ["%s%d" % (s, b) for s in BLOCKS for b in range(NB)]
+              + ["lx0", "lx1", "lw1", "lw2", "one", "idn", "sp", "qw2", "left", "sent", "sth", "sty"])
 
 
 def _bits(mask):
@@ -67,34 +67,56 @@ def _plan(T, topo):
     return plan
 
 
-def _piece(q, s, i):
-    if i < NS:
-        return q[:, SW * i:SW * i + SW].bitcast(dt.uint8)
-    return s[:]
+def _codes(q, c):
+    return q[:, SW * c:SW * c + SW].bitcast(dt.uint8)
+
+
+def _plane(s, c):
+    return s[:, SW * c:SW * c + SW]
 
 
 def _helper(g, core, T, topo, src, dst, which):
     rid, pid = topo.addr(dst, core)
     out_mask = topo.mask(core, dst)
     landed = len(_bits(topo.mask(src, core))) // 2
-    mine = [i for i in range(NS + 1) if ROUTE[i] == which]
-    for i in mine:
-        g.wait_ge(T.sem["in%d" % i], landed)
-        g.remote_dma(out_ap=_piece(T.rq, T.rs, i), in_ap=_piece(T.rq, T.rs, i), remote_sem=T.sem.arr,
+    for c in range(NS):
+        if c % 2 == which:
+            g.wait_ge(T.sem["ic%d" % c], landed)
+            out_ap, in_ap = _codes(T.rq, c), _codes(T.rq, c)
+        else:
+            g.wait_ge(T.sem["ip%d" % c], landed)
+            out_ap, in_ap = _plane(T.rs, c), _plane(T.rs, c)
+        g.remote_dma(out_ap=out_ap, in_ap=in_ap, remote_sem=T.sem["arr%d" % c],
                      local_sem=T.sem.sent, pid=pid, routing_id=rid, dma_engine_mask=out_mask)
-    g.wait_ge(T.sem.sent, len(_bits(out_mask)) * len(mine))
+    g.wait_ge(T.sem.sent, len(_bits(out_mask)) * NS)
 
 
 def _rank(g, core, T, topo, helpers, arrivals):
     S = T.sem
     AF, OP = ActivationFunctionType, AluOpType
     ve, te, sc, sy = g.vector, g.tensor, g.scalar, g.sync
+    last = NS - 1
 
     def col(k, c):
         return T.st[:, NS * k + c:NS * k + c + 1]
 
     def sl(t, c, w):
         return t[:, w * c:w * c + w]
+
+    def bank(b):
+        return T.pe[:, BANK * b:BANK * b + SW]
+
+    def prod(c):
+        return T.zp[:, BANK * (c - 1):BANK * c]
+
+    def prod_b(c, b):
+        return T.zp[:, BANK * (c - 1) + SW * b:BANK * (c - 1) + SW * b + SW]
+
+    def turned(c, b):
+        return T.rt[:, 4 * SW * c + SW * b:4 * SW * c + SW * b + SW]
+
+    def h_cols(c, b):
+        return T.ht[:, 4 * SW * c + b:4 * SW * (c + 1):4]
 
     sy.dma_start(T.xt[:, 0:4 * SW], T.x[:, 0:4 * SW]).then_inc(S.lx0, 16)
     sc.dma_start(T.w1t[:], T.w1[:]).then_inc(S.lw1, 16)
@@ -108,7 +130,7 @@ def _rank(g, core, T, topo, helpers, arrivals):
     def pack_x(c):
         ve.quantize_mx(sl(T.xq, c, SW), sl(T.xs, c, SW), sl(T.xt, c, 4 * SW)).then_inc(S["qx%d" % c], 1)
 
-    def norm(c):
+    def factors(c):
         ve.wait_ge(S["sq%d" % c], 1)
         ve.tensor_scalar(col(2, c), col(0, c), 1.0 / ROWS, EPS, OP.mult, OP.add).then_inc(S["vv%d" % c], 1)
         ve.wait_ge(S["ro%d" % c], 1)
@@ -119,87 +141,113 @@ def _rank(g, core, T, topo, helpers, arrivals):
         ve.wait_ge(S["nt%d" % c], 1)
         ve.tensor_scalar(col(5, c), col(4, c), -0.5, 1.5, OP.mult, OP.add).then_inc(S["nu%d" % c], 1)
         ve.wait_ge(S["nu%d" % c], 1)
+
+    def scale(c):
         ve.wait_ge(S["mx%d" % c], 1)
-        ve.tensor_scalar(sl(T.rt, c, 4 * SW), sl(T.zp, c, 4 * SW), col(3, c), col(5, c),
-                         OP.mult, OP.mult).then_inc(S["sc%d" % c], 1)
+        ve.tensor_scalar(sl(T.rt, c, 4 * SW), prod(c), col(3, c), col(5, c), OP.mult, OP.mult).then_inc(S["sc%d" % c], 1)
 
     def pack_h(c):
-        ve.wait_ge(S["cp%d" % c], 4)
+        ve.wait_ge(S["cp%d" % c], NB)
         ve.quantize_mx(sl(T.hq, c, SW), sl(T.hs, c, SW), sl(T.ht, c, 4 * SW)).then_inc(S["qh%d" % c], 1)
 
-    def h_cols(c, b):
-        return T.ht[:, 4 * SW * c + b:4 * SW * (c + 1):4]
-
-    last = NS - 1
     ve.wait_ge(S.lx0, 16)
     pack_x(0)
     ve.wait_ge(S.lw1, 16)
-    ve.quantize_mx(T.w1q[:], T.w1s[:], T.w1t[:]).then_inc(S.qw1, 1)
+    for b in range(NB):
+        ve.quantize_mx(sl(T.w1q, b, SW), sl(T.w1s, b, SW), sl(T.w1t, b, 4 * SW)).then_inc(S["wq%d" % b], 1)
     ve.wait_ge(S.lx1, 16)
     for c in range(1, NS):
         pack_x(c)
-    norm(0)
-    for c in range(1, NS):
-        norm(c)
-        pack_h(c - 1)
-    ve.wait_ge(S["tr%d" % last], 2)
-    for b in (0, 1):
-        ve.tensor_copy(h_cols(last, b), T.zp[:, 4 * SW * last + SW * b:4 * SW * last + SW * b + SW]).then_inc(S["cp%d" % last], 1)
+    factors(0)
+    for b in range(NB):
+        ve.wait_ge(S["ma%d" % b], 1)
+        ve.tensor_scalar(turned(0, b), bank(b), col(3, 0), col(5, 0), OP.mult, OP.mult).then_inc(S["sa%d" % b], 1)
+    factors(1)
+    scale(1)
+    pack_h(0)
+    factors(2)
+    scale(2)
+    factors(last)
+    pack_h(1)
+    ve.wait_ge(S["mx%d" % last], 1)
+    for b in range(NB):
+        ve.tensor_scalar(turned(last, b), prod_b(last, b), col(3, last), col(5, last),
+                         OP.mult, OP.mult).then_inc(S["sz%d" % b], 1)
+    pack_h(2)
+    ve.wait_ge(S["tz%d" % (NB - 1)], 1)
+    ve.tensor_copy(h_cols(last, NB - 1), bank(NB - 1)).then_inc(S["cp%d" % last], 1)
     pack_h(last)
     ve.wait_ge(S.lw2, 16)
     ve.quantize_mx(T.w2q[:], T.w2s[:], T.w2t[:]).then_inc(S.qw2, 1)
-    ve.wait_ge(S.ya, 1)
-    ve.tensor_copy(T.yt[:, 0:256], T.yp[:, 0:256]).then_inc(S.cy, 1)
+    for c in range(0, NS, 2):
+        ve.wait_ge(S["ym%d" % c], 1)
+        ve.tensor_copy(sl(T.yt, c, SW), bank(c)).then_inc(S["cy%d" % c], 1)
 
-    def stats(c):
-        sc.wait_ge(S["mx%d" % c], 1)
-        sc.activation(T.sqr[:], sl(T.zp, c, 4 * SW), AF.Square, accum_out=col(0, c)).then_inc(S["sq%d" % c], 1)
+    def root(c):
         sc.wait_ge(S["sq%d" % c], 1)
         sc.activation(col(1, c), col(0, c), AF.Sqrt, bias=EPS, scale=1.0 / ROWS).then_inc(S["ro%d" % c], 1)
 
-    def back(c):
-        sc.wait_ge(S["tr%d" % c], 4)
-        for b in range(4):
-            sc.activation(h_cols(c, b), T.zp[:, 4 * SW * c + SW * b:4 * SW * c + SW * b + SW], AF.Copy).then_inc(S["cp%d" % c], 1)
+    def stats(c):
+        sc.wait_ge(S["mx%d" % c], 1)
+        sc.activation(T.sqr[:], prod(c), AF.Square, accum_out=col(0, c)).then_inc(S["sq%d" % c], 1)
+        root(c)
 
-    stats(0)
+    def back(c):
+        sc.wait_ge(S["tr%d" % c], NB)
+        for b in range(NB):
+            sc.activation(h_cols(c, b), prod_b(c, b), AF.Copy).then_inc(S["cp%d" % c], 1)
+
+    part = 6 * NS
+    for b in range(NB):
+        sc.wait_ge(S["ma%d" % b], 1)
+        sc.activation(sl(T.sqr, b, SW), bank(b), AF.Square, accum_out=T.st[:, part + b:part + b + 1]).then_inc(S.sp, 1)
+    sc.wait_ge(S.sp, NB)
+    sc.activation(T.st[:, part + NB:part + 2 * NB], T.st[:, part:part + NB], AF.Copy, accum_out=col(0, 0)).then_inc(S.sq0, 1)
+    root(0)
     stats(1)
     stats(2)
-    back(0)
-    stats(3)
+    for b in range(NB):
+        sc.wait_ge(S["ta%d" % b], 1)
+        sc.activation(h_cols(0, b), bank(b), AF.Copy).then_inc(S.cp0, 1)
+    stats(last)
     back(1)
     back(2)
-    sc.wait_ge(S.te, 2)
-    for b in (2, 3):
-        sc.activation(h_cols(last, b), T.ze[:, SW * (b - 2):SW * (b - 1)], AF.Copy).then_inc(S["cp%d" % last], 1)
-    sc.wait_ge(S.yb, 1)
-    sc.activation(T.yt[:, 256:512], T.yp[:, 512:768], AF.Copy).then_inc(S.cy, 1)
+    for b in range(NB - 1):
+        sc.wait_ge(S["tz%d" % b], 1)
+        sc.activation(h_cols(last, b), bank(b), AF.Copy).then_inc(S["cp%d" % last], 1)
+    for c in range(1, NS, 2):
+        sc.wait_ge(S["ym%d" % c], 1)
+        sc.activation(sl(T.yt, c, SW), bank(c), AF.Copy).then_inc(S["cy%d" % c], 1)
 
-    te.wait_ge(S.qw1, 1)
-    for c in range(NS):
+    te.wait_ge(S.qx0, 1)
+    for b in range(NB):
+        te.wait_ge(S["wq%d" % b], 1)
+        te.matmul_mx(bank(b), sl(T.xq, 0, SW), sl(T.xs, 0, SW), sl(T.w1q, b, SW), sl(T.w1s, b, SW),
+                     True, True).then_inc(S["ma%d" % b], 1)
+    for c in range(1, NS):
         te.wait_ge(S["qx%d" % c], 1)
-        te.matmul_mx(sl(T.zp, c, 4 * SW), sl(T.xq, c, SW), sl(T.xs, c, SW), T.w1q[:], T.w1s[:],
-                     True, True).then_inc(S["mx%d" % c], 1)
+        te.matmul_mx(prod(c), sl(T.xq, c, SW), sl(T.xs, c, SW), T.w1q[:], T.w1s[:], True, True).then_inc(S["mx%d" % c], 1)
     te.wait_ge(S.idn, 1)
-    for c in range(NS):
+    for b in range(NB):
+        te.wait_ge(S["sa%d" % b], 1)
+        te.matmul(bank(b), turned(0, b), T.ident[:], True, True).then_inc(S["ta%d" % b], 1)
+    for c in range(1, last):
         te.wait_ge(S["sc%d" % c], 1)
-        for b in range(4):
-            turned = T.rt[:, 4 * SW * c + SW * b:4 * SW * c + SW * b + SW]
-            if c == last and b >= 2:
-                te.matmul(T.ze[:, SW * (b - 2):SW * (b - 1)], turned, T.ident[:], True, True).then_inc(S.te, 1)
-            else:
-                te.matmul(T.zp[:, 4 * SW * c + SW * b:4 * SW * c + SW * b + SW], turned, T.ident[:],
-                          True, True).then_inc(S["tr%d" % c], 1)
+        for b in range(NB):
+            te.matmul(prod_b(c, b), turned(c, b), T.ident[:], True, True).then_inc(S["tr%d" % c], 1)
+    te.wait_ge(S.cp0, NB)
+    for b in range(NB):
+        te.wait_ge(S["sz%d" % b], 1)
+        te.matmul(bank(b), turned(last, b), T.ident[:], True, True).then_inc(S["tz%d" % b], 1)
     te.wait_ge(S.qw2, 1)
     for c in range(NS):
         te.wait_ge(S["qh%d" % c], 1)
-    for k in range(2):
-        te.matmul_mx(T.yp[:, 512 * k:512 * k + 256], T.w2q[:, 0:128], T.w2s[:, 0:128],
-                     T.hq[:, 256 * k:256 * k + 256], T.hs[:, 256 * k:256 * k + 256], True, False)
-    te.wait_ge(S.arr, arrivals)
-    for k in range(2):
-        te.matmul_mx(T.yp[:, 512 * k:512 * k + 256], T.w2q[:, 128:256], T.w2s[:, 128:256],
-                     T.rq[:, 256 * k:256 * k + 256], T.rs[:, 256 * k:256 * k + 256], False, True).then_inc((S.ya, S.yb)[k], 1)
+    for c in range(NS):
+        te.matmul_mx(bank(c), T.w2q[:, 0:128], T.w2s[:, 0:128], sl(T.hq, c, SW), sl(T.hs, c, SW), True, False)
+    for c in range(NS):
+        te.wait_ge(S["arr%d" % c], arrivals)
+        te.matmul_mx(bank(c), T.w2q[:, 128:256], T.w2s[:, 128:256], sl(T.rq, c, SW), sl(T.rs, c, SW),
+                     False, True).then_inc(S["ym%d" % c], 1)
 
     where, engines = [], []
     for k in range(2):
@@ -208,29 +256,24 @@ def _rank(g, core, T, topo, helpers, arrivals):
         half = len(bits) // 2
         engines.append(_mask(bits[half * k:half * k + half]))
     left = 0
-    for i in range(NS - 1):
-        k = ROUTE[i]
-        g.wait_ge(S["qh%d" % i], 1)
-        g.remote_dma(out_ap=_piece(T.rq, T.rs, i), in_ap=_piece(T.hq, T.hs, i), remote_sem=S["in%d" % i],
+    for c in range(NS):
+        k = c % 2
+        g.wait_ge(S["qh%d" % c], 1)
+        g.remote_dma(out_ap=_codes(T.rq, c), in_ap=_codes(T.hq, c), remote_sem=S["ic%d" % c],
                      local_sem=S.left, pid=where[k][1], routing_id=where[k][0], dma_engine_mask=engines[k])
-        left += len(_bits(engines[k]))
-    g.wait_ge(S["qh%d" % last], 1)
-    both = []
-    for i in (NS - 1, NS):
-        k = ROUTE[i]
-        both.append(RemoteDMATransfer(dst_ids=[DstId(rid=where[k][0], pnc=where[k][1])], dma_engine_mask=engines[k],
-                                      remote_sem=S["in%d" % i], src=_piece(T.hq, T.hs, i), dst=_piece(T.rq, T.rs, i)))
-        left += len(_bits(engines[k]))
-    g.remote_dma_fused(both, local_sem=S.left)
+        g.remote_dma(out_ap=_plane(T.rs, c), in_ap=_plane(T.hs, c), remote_sem=S["ip%d" % c],
+                     local_sem=S.left, pid=where[1 - k][1], routing_id=where[1 - k][0], dma_engine_mask=engines[1 - k])
+        left += len(_bits(engines[k])) + len(_bits(engines[1 - k]))
 
     for c in range(NS):
-        sy.wait_ge(S["cp%d" % c], 4)
+        sy.wait_ge(S["cp%d" % c], NB)
     sy.wait_ge(S.left, left)
     sy.dma_start(T.h[:], T.ht[:]).then_inc(S.sth, 16)
-    sy.wait_ge(S.cy, 2)
-    sy.dma_start(T.y[:], T.yt[:]).then_inc(S.sty, 16)
+    for c in range(NS):
+        sy.wait_ge(S["cy%d" % c], 1)
+        sy.dma_start(sl(T.y, c, SW), sl(T.yt, c, SW)).then_inc(S.sty, 16)
     sy.wait_ge(S.sth, 16)
-    sy.wait_ge(S.sty, 16)
+    sy.wait_ge(S.sty, 16 * NS)
 
 
 def rank_program(g, core, T, topo):
@@ -239,7 +282,7 @@ def rank_program(g, core, T, topo):
     rank = T.rank_of(core)
     if rank is not None:
         src, dst, helpers = plan[(rank + 1) % n]
-        arrivals = sum(len(_bits(topo.mask(helpers[ROUTE[i]], dst))) for i in range(NS + 1))
+        arrivals = sum(len(_bits(topo.mask(h, dst))) for h in helpers)
         _rank(g, core, T, topo, plan[rank][2], arrivals)
         return
     for src, dst, helpers in plan:

@@ -20,7 +20,7 @@ SCRATCH = {
     "w2s": ("sbuf", [128, 256], "uint8"),
     "ident": ("sbuf", [128, 128], "bfloat16"),
     "sqr": ("sbuf", [128, 512], "float32"),
-    "st": ("sbuf", [128, 32], "float32"),
+    "st": ("sbuf", [128, 40], "float32"),
     "rt": ("sbuf", [128, 2048], "bfloat16"),
     "ht": ("sbuf", [128, 2048], "bfloat16"),
     "hq": ("sbuf", [128, 512], "float8_e4m3fn_x4"),
@@ -31,22 +31,17 @@ SCRATCH = {
     "pe": ("psum", [128, 2048], "float32"),
     "zp": ("psum", [128, 1536], "float32"),
 }
-STAGES = ("qx", "mx", "sq", "ro", "vv", "rc", "nt", "nu", "sc", "tr", "cp", "qh", "ic", "ip", "arr", "ym", "cy")
-BLOCKS = ("wq", "ma", "sa", "ta", "sz", "tz")
-SEMAPHORES = (["%s%d" % (s, c) for s in STAGES for c in range(NS)]
+SLICES = ("qx", "mx", "sq", "ro", "ww", "vv", "rc", "nu", "qh", "ic", "ip", "arr", "ym", "cy")
+PIECES = ("sc", "tr", "cp")
+BLOCKS = ("wq", "ma")
+SEMAPHORES = (["%s%d" % (s, c) for s in SLICES for c in range(NS)]
+              + ["%s%d%d" % (s, c, b) for s in PIECES for c in range(NS) for b in range(NB)]
               + ["%s%d" % (s, b) for s in BLOCKS for b in range(NB)]
-              + ["lx0", "lx1", "lw1", "lw2", "one", "idn", "sp", "qw2", "left", "sent", "sth", "sty"])
+              + ["lx0", "lx1", "lwa", "lwb", "lw2", "one", "idn", "sp", "qw2", "lefta", "leftb", "sent", "sth", "sty"])
 
 
 def _bits(mask):
     return [i for i in range(mask.bit_length()) if (mask >> i) & 1]
-
-
-def _mask(bits):
-    m = 0
-    for i in bits:
-        m |= 1 << i
-    return m
 
 
 def _plan(T, topo):
@@ -59,46 +54,58 @@ def _plan(T, topo):
         cand = [c for c in world
                 if topo.host(c) == topo.host(src) and topo.chip(c) == topo.chip(src) and c not in cores
                 and topo.may_write(src, c) and topo.may_write(c, dst)]
-        near = [c for c in cand if topo.die(c) == topo.die(src)]
-        far = [c for c in cand if topo.die(c) != topo.die(src)]
-        first = (near + far)[0]
-        second = [c for c in far + near if c != first][0]
-        plan.append((src, dst, (first, second)))
+        near = [c for c in cand if topo.die(c) == topo.die(src)] or cand
+        far = [c for c in cand if topo.die(c) != topo.die(src)] or cand
+        route = []
+        for c in range(NS):
+            own, other = (near[0], far[-1]), (far[0], near[-1])
+            if (NS - 1 - c) % 2:
+                own, other = other, own
+            if c == 0:
+                m = SW // 2
+                route.append([(0, 0, m, own[0]), (0, m, SW, other[0]), (1, 0, m, own[1]), (1, m, SW, other[1])])
+            else:
+                route.append([(0, 0, SW, own[0]), (1, 0, SW, own[1])])
+        plan.append((src, dst, route))
     return plan
 
 
-def _codes(q, c):
-    return q[:, SW * c:SW * c + SW].bitcast(dt.uint8)
+def _piece(q, s, c, kind, lo, hi):
+    if kind == 0:
+        return q[:, SW * c + lo:SW * c + hi].bitcast(dt.uint8)
+    return s[:, SW * c + lo:SW * c + hi]
 
 
-def _plane(s, c):
-    return s[:, SW * c:SW * c + SW]
-
-
-def _helper(g, core, T, topo, src, dst, which):
+def _helper(g, core, T, topo, src, dst, route):
     rid, pid = topo.addr(dst, core)
     out_mask = topo.mask(core, dst)
-    landed = len(_bits(topo.mask(src, core))) // 2
+    landed = len(_bits(topo.mask(src, core)))
+    sent = 0
     for c in range(NS):
-        if c % 2 == which:
-            g.wait_ge(T.sem["ic%d" % c], landed)
-            out_ap, in_ap = _codes(T.rq, c), _codes(T.rq, c)
-        else:
-            g.wait_ge(T.sem["ip%d" % c], landed)
-            out_ap, in_ap = _plane(T.rs, c), _plane(T.rs, c)
-        g.remote_dma(out_ap=out_ap, in_ap=in_ap, remote_sem=T.sem["arr%d" % c],
-                     local_sem=T.sem.sent, pid=pid, routing_id=rid, dma_engine_mask=out_mask)
-    g.wait_ge(T.sem.sent, len(_bits(out_mask)) * NS)
+        for kind, lo, hi, by in route[c]:
+            if by != core:
+                continue
+            g.wait_ge(T.sem["%s%d" % (("ic", "ip")[kind], c)], landed)
+            ap = _piece(T.rq, T.rs, c, kind, lo, hi)
+            g.remote_dma(out_ap=ap, in_ap=ap, remote_sem=T.sem["arr%d" % c],
+                         local_sem=T.sem.sent, pid=pid, routing_id=rid, dma_engine_mask=out_mask)
+            sent += len(_bits(out_mask))
+    g.wait_ge(T.sem.sent, sent)
 
 
-def _rank(g, core, T, topo, helpers, arrivals):
+def _rank(g, core, T, topo, route, arrivals):
     S = T.sem
     AF, OP = ActivationFunctionType, AluOpType
     ve, te, sc, sy = g.vector, g.tensor, g.scalar, g.sync
     last = NS - 1
+    half = NS // 2
 
     def col(k, c):
         return T.st[:, NS * k + c:NS * k + c + 1]
+
+    def duo(k, c, i, n):
+        at = 3 * NS + 2 * NS * k + 2 * c + i
+        return T.st[:, at:at + n]
 
     def sl(t, c, w):
         return t[:, w * c:w * c + w]
@@ -110,7 +117,7 @@ def _rank(g, core, T, topo, helpers, arrivals):
         return T.zp[:, BANK * (c - 1):BANK * c]
 
     def prod_b(c, b):
-        return T.zp[:, BANK * (c - 1) + SW * b:BANK * (c - 1) + SW * b + SW]
+        return bank(b) if c == 0 else T.zp[:, BANK * (c - 1) + SW * b:BANK * (c - 1) + SW * b + SW]
 
     def turned(c, b):
         return T.rt[:, 4 * SW * c + SW * b:4 * SW * c + SW * b + SW]
@@ -118,10 +125,12 @@ def _rank(g, core, T, topo, helpers, arrivals):
     def h_cols(c, b):
         return T.ht[:, 4 * SW * c + b:4 * SW * (c + 1):4]
 
+    hw = 2 * 4 * SW
     sy.dma_start(T.xt[:, 0:4 * SW], T.x[:, 0:4 * SW]).then_inc(S.lx0, 16)
-    sc.dma_start(T.w1t[:], T.w1[:]).then_inc(S.lw1, 16)
+    sc.dma_start(T.w1t[:, 0:hw], T.w1[:, 0:hw]).then_inc(S.lwa, 16)
+    sy.dma_start(T.w1t[:, hw:], T.w1[:, hw:]).then_inc(S.lwb, 16)
     sy.dma_start(T.xt[:, 4 * SW:], T.x[:, 4 * SW:]).then_inc(S.lx1, 16)
-    sc.dma_start(T.w2t[:], T.w2[:]).then_inc(S.lw2, 16)
+    sy.dma_start(T.w2t[:], T.w2[:]).then_inc(S.lw2, 16)
 
     ve.memset(T.ident[:], 1.0).then_inc(S.one, 1)
     g.wait_ge(S.one, 1)
@@ -131,37 +140,33 @@ def _rank(g, core, T, topo, helpers, arrivals):
         ve.quantize_mx(sl(T.xq, c, SW), sl(T.xs, c, SW), sl(T.xt, c, 4 * SW)).then_inc(S["qx%d" % c], 1)
 
     def factors(c):
-        ve.wait_ge(S["sq%d" % c], 1)
-        ve.tensor_scalar(col(2, c), col(0, c), 1.0 / ROWS, EPS, OP.mult, OP.add).then_inc(S["vv%d" % c], 1)
-        ve.wait_ge(S["ro%d" % c], 1)
-        ve.reciprocal(col(3, c), col(1, c)).then_inc(S["rc%d" % c], 1)
+        ve.wait_ge(S["ww%d" % c], 1)
+        ve.reciprocal(duo(1, c, 0, 2), duo(0, c, 0, 2)).then_inc(S["rc%d" % c], 1)
         ve.wait_ge(S["vv%d" % c], 1)
         ve.wait_ge(S["rc%d" % c], 1)
-        ve.tensor_scalar(col(4, c), col(3, c), col(3, c), col(2, c), OP.mult, OP.mult).then_inc(S["nt%d" % c], 1)
-        ve.wait_ge(S["nt%d" % c], 1)
-        ve.tensor_scalar(col(5, c), col(4, c), -0.5, 1.5, OP.mult, OP.add).then_inc(S["nu%d" % c], 1)
+        ve.tensor_scalar(col(2, c), duo(1, c, 1, 1), col(1, c), 1.5, OP.mult, OP.add).then_inc(S["nu%d" % c], 1)
         ve.wait_ge(S["nu%d" % c], 1)
 
     def scale(c):
-        ve.wait_ge(S["mx%d" % c], 1)
-        ve.tensor_scalar(sl(T.rt, c, 4 * SW), prod(c), col(3, c), col(5, c), OP.mult, OP.mult).then_inc(S["sc%d" % c], 1)
+        for b in range(NB):
+            ve.wait_ge(S["ma%d" % b] if c == 0 else S["mx%d" % c], 1)
+            ve.tensor_scalar(turned(c, b), prod_b(c, b), duo(1, c, 0, 1), col(2, c), OP.mult, OP.mult).then_inc(S["sc%d%d" % (c, b)], 1)
 
     def pack_h(c):
-        ve.wait_ge(S["cp%d" % c], NB)
+        for b in range(NB):
+            ve.wait_ge(S["cp%d%d" % (c, b)], 1)
         ve.quantize_mx(sl(T.hq, c, SW), sl(T.hs, c, SW), sl(T.ht, c, 4 * SW)).then_inc(S["qh%d" % c], 1)
 
     ve.wait_ge(S.lx0, 16)
     pack_x(0)
-    ve.wait_ge(S.lw1, 16)
     for b in range(NB):
+        ve.wait_ge(S.lwa if b < NB // 2 else S.lwb, 16)
         ve.quantize_mx(sl(T.w1q, b, SW), sl(T.w1s, b, SW), sl(T.w1t, b, 4 * SW)).then_inc(S["wq%d" % b], 1)
     ve.wait_ge(S.lx1, 16)
     for c in range(1, NS):
         pack_x(c)
     factors(0)
-    for b in range(NB):
-        ve.wait_ge(S["ma%d" % b], 1)
-        ve.tensor_scalar(turned(0, b), bank(b), col(3, 0), col(5, 0), OP.mult, OP.mult).then_inc(S["sa%d" % b], 1)
+    scale(0)
     factors(1)
     scale(1)
     pack_h(0)
@@ -169,13 +174,10 @@ def _rank(g, core, T, topo, helpers, arrivals):
     scale(2)
     factors(last)
     pack_h(1)
-    ve.wait_ge(S["mx%d" % last], 1)
-    for b in range(NB):
-        ve.tensor_scalar(turned(last, b), prod_b(last, b), col(3, last), col(5, last),
-                         OP.mult, OP.mult).then_inc(S["sz%d" % b], 1)
+    scale(last)
     pack_h(2)
-    ve.wait_ge(S["tz%d" % (NB - 1)], 1)
-    ve.tensor_copy(h_cols(last, NB - 1), bank(NB - 1)).then_inc(S["cp%d" % last], 1)
+    ve.wait_ge(S["tr%d%d" % (last, NB - 1)], 1)
+    ve.tensor_copy(h_cols(last, NB - 1), bank(NB - 1)).then_inc(S["cp%d%d" % (last, NB - 1)], 1)
     pack_h(last)
     ve.wait_ge(S.lw2, 16)
     ve.quantize_mx(T.w2q[:], T.w2s[:], T.w2t[:]).then_inc(S.qw2, 1)
@@ -185,19 +187,22 @@ def _rank(g, core, T, topo, helpers, arrivals):
 
     def root(c):
         sc.wait_ge(S["sq%d" % c], 1)
-        sc.activation(col(1, c), col(0, c), AF.Sqrt, bias=EPS, scale=1.0 / ROWS).then_inc(S["ro%d" % c], 1)
+        sc.activation(duo(0, c, 0, 1), col(0, c), AF.Sqrt, bias=EPS, scale=1.0 / ROWS).then_inc(S["ro%d" % c], 1)
+        sc.wait_ge(S["ro%d" % c], 1)
+        sc.activation(duo(0, c, 1, 1), duo(0, c, 0, 1), AF.Square).then_inc(S["ww%d" % c], 1)
+        sc.activation(col(1, c), col(0, c), AF.Identity, bias=-0.5 * EPS, scale=-0.5 / ROWS).then_inc(S["vv%d" % c], 1)
 
     def stats(c):
         sc.wait_ge(S["mx%d" % c], 1)
         sc.activation(T.sqr[:], prod(c), AF.Square, accum_out=col(0, c)).then_inc(S["sq%d" % c], 1)
         root(c)
 
-    def back(c):
-        sc.wait_ge(S["tr%d" % c], NB)
-        for b in range(NB):
-            sc.activation(h_cols(c, b), prod_b(c, b), AF.Copy).then_inc(S["cp%d" % c], 1)
+    def back(c, blocks):
+        for b in blocks:
+            sc.wait_ge(S["tr%d%d" % (c, b)], 1)
+            sc.activation(h_cols(c, b), bank(b), AF.Copy).then_inc(S["cp%d%d" % (c, b)], 1)
 
-    part = 6 * NS
+    part = 7 * NS
     for b in range(NB):
         sc.wait_ge(S["ma%d" % b], 1)
         sc.activation(sl(T.sqr, b, SW), bank(b), AF.Square, accum_out=T.st[:, part + b:part + b + 1]).then_inc(S.sp, 1)
@@ -206,15 +211,11 @@ def _rank(g, core, T, topo, helpers, arrivals):
     root(0)
     stats(1)
     stats(2)
-    for b in range(NB):
-        sc.wait_ge(S["ta%d" % b], 1)
-        sc.activation(h_cols(0, b), bank(b), AF.Copy).then_inc(S.cp0, 1)
+    back(0, range(NB))
     stats(last)
-    back(1)
-    back(2)
-    for b in range(NB - 1):
-        sc.wait_ge(S["tz%d" % b], 1)
-        sc.activation(h_cols(last, b), bank(b), AF.Copy).then_inc(S["cp%d" % last], 1)
+    back(1, range(NB))
+    back(2, range(NB))
+    back(last, range(NB - 1))
     for c in range(1, NS, 2):
         sc.wait_ge(S["ym%d" % c], 1)
         sc.activation(sl(T.yt, c, SW), bank(c), AF.Copy).then_inc(S["cy%d" % c], 1)
@@ -228,51 +229,46 @@ def _rank(g, core, T, topo, helpers, arrivals):
         te.wait_ge(S["qx%d" % c], 1)
         te.matmul_mx(prod(c), sl(T.xq, c, SW), sl(T.xs, c, SW), T.w1q[:], T.w1s[:], True, True).then_inc(S["mx%d" % c], 1)
     te.wait_ge(S.idn, 1)
-    for b in range(NB):
-        te.wait_ge(S["sa%d" % b], 1)
-        te.matmul(bank(b), turned(0, b), T.ident[:], True, True).then_inc(S["ta%d" % b], 1)
-    for c in range(1, last):
-        te.wait_ge(S["sc%d" % c], 1)
+    for c in range(NS):
         for b in range(NB):
-            te.matmul(prod_b(c, b), turned(c, b), T.ident[:], True, True).then_inc(S["tr%d" % c], 1)
-    te.wait_ge(S.cp0, NB)
-    for b in range(NB):
-        te.wait_ge(S["sz%d" % b], 1)
-        te.matmul(bank(b), turned(last, b), T.ident[:], True, True).then_inc(S["tz%d" % b], 1)
+            te.wait_ge(S["sc%d%d" % (c, b)], 1)
+            if c:
+                te.wait_ge(S["cp%d%d" % (c - 1, b)], 1)
+            te.matmul(bank(b), turned(c, b), T.ident[:], True, True).then_inc(S["tr%d%d" % (c, b)], 1)
     te.wait_ge(S.qw2, 1)
     for c in range(NS):
         te.wait_ge(S["qh%d" % c], 1)
     for c in range(NS):
         te.matmul_mx(bank(c), T.w2q[:, 0:128], T.w2s[:, 0:128], sl(T.hq, c, SW), sl(T.hs, c, SW), True, False)
     for c in range(NS):
-        te.wait_ge(S["arr%d" % c], arrivals)
+        te.wait_ge(S["arr%d" % c], arrivals[c])
         te.matmul_mx(bank(c), T.w2q[:, 128:256], T.w2s[:, 128:256], sl(T.rq, c, SW), sl(T.rs, c, SW),
                      False, True).then_inc(S["ym%d" % c], 1)
 
-    where, engines = [], []
-    for k in range(2):
-        where.append(topo.addr(helpers[k], core))
-        bits = _bits(topo.mask(core, helpers[k]))
-        half = len(bits) // 2
-        engines.append(_mask(bits[half * k:half * k + half]))
-    left = 0
+    left = [0, 0]
     for c in range(NS):
-        k = c % 2
         g.wait_ge(S["qh%d" % c], 1)
-        g.remote_dma(out_ap=_codes(T.rq, c), in_ap=_codes(T.hq, c), remote_sem=S["ic%d" % c],
-                     local_sem=S.left, pid=where[k][1], routing_id=where[k][0], dma_engine_mask=engines[k])
-        g.remote_dma(out_ap=_plane(T.rs, c), in_ap=_plane(T.hs, c), remote_sem=S["ip%d" % c],
-                     local_sem=S.left, pid=where[1 - k][1], routing_id=where[1 - k][0], dma_engine_mask=engines[1 - k])
-        left += len(_bits(engines[k])) + len(_bits(engines[1 - k]))
+        for kind, lo, hi, to in route[c]:
+            rid, pid = topo.addr(to, core)
+            engines = topo.mask(core, to)
+            g.remote_dma(out_ap=_piece(T.rq, T.rs, c, kind, lo, hi), in_ap=_piece(T.hq, T.hs, c, kind, lo, hi),
+                         remote_sem=S["%s%d" % (("ic", "ip")[kind], c)],
+                         local_sem=S.lefta if c < half else S.leftb, pid=pid, routing_id=rid, dma_engine_mask=engines)
+            left[c // half] += len(_bits(engines))
 
-    for c in range(NS):
-        sy.wait_ge(S["cp%d" % c], NB)
-    sy.wait_ge(S.left, left)
-    sy.dma_start(T.h[:], T.ht[:]).then_inc(S.sth, 16)
+    hh = 4 * SW * half
+    for c in range(half):
+        sy.wait_ge(S["qh%d" % c], 1)
+    sy.wait_ge(S.lefta, left[0])
+    sy.dma_start(T.h[:, 0:hh], T.ht[:, 0:hh]).then_inc(S.sth, 16)
+    for c in range(half, NS):
+        sy.wait_ge(S["qh%d" % c], 1)
+    sy.wait_ge(S.leftb, left[1])
+    sy.dma_start(T.h[:, hh:], T.ht[:, hh:]).then_inc(S.sth, 16)
     for c in range(NS):
         sy.wait_ge(S["cy%d" % c], 1)
         sy.dma_start(sl(T.y, c, SW), sl(T.yt, c, SW)).then_inc(S.sty, 16)
-    sy.wait_ge(S.sth, 16)
+    sy.wait_ge(S.sth, 32)
     sy.wait_ge(S.sty, 16 * NS)
 
 
@@ -281,11 +277,10 @@ def rank_program(g, core, T, topo):
     n = len(plan)
     rank = T.rank_of(core)
     if rank is not None:
-        src, dst, helpers = plan[(rank + 1) % n]
-        arrivals = sum(len(_bits(topo.mask(h, dst))) for h in helpers)
+        src, dst, route = plan[(rank + 1) % n]
+        arrivals = [sum(len(_bits(topo.mask(p[3], dst))) for p in route[c]) for c in range(NS)]
         _rank(g, core, T, topo, plan[rank][2], arrivals)
         return
-    for src, dst, helpers in plan:
-        for k in range(2):
-            if helpers[k] == core:
-                _helper(g, core, T, topo, src, dst, k)
+    for src, dst, route in plan:
+        if any(p[3] == core for pieces in route for p in pieces):
+            _helper(g, core, T, topo, src, dst, route)

from concourse.bass import DstId, RemoteDMATransfer
from concourse.mybir import dt, AluOpType, ActivationFunctionType

NS = 4
NB = 4
SW = 128
BANK = 512
EPS = 0.001
ROWS = 512

SCRATCH = {
    "xt": ("sbuf", [128, 2048], "bfloat16"),
    "w1t": ("sbuf", [128, 2048], "bfloat16"),
    "w2t": ("sbuf", [128, 1024], "bfloat16"),
    "xq": ("sbuf", [128, 512], "float8_e4m3fn_x4"),
    "xs": ("sbuf", [128, 512], "uint8"),
    "w1q": ("sbuf", [128, 512], "float8_e4m3fn_x4"),
    "w1s": ("sbuf", [128, 512], "uint8"),
    "w2q": ("sbuf", [128, 256], "float8_e4m3fn_x4"),
    "w2s": ("sbuf", [128, 256], "uint8"),
    "ident": ("sbuf", [128, 128], "bfloat16"),
    "sqr": ("sbuf", [128, 512], "float32"),
    "st": ("sbuf", [128, 40], "float32"),
    "rt": ("sbuf", [128, 2048], "bfloat16"),
    "ht": ("sbuf", [128, 2048], "bfloat16"),
    "hq": ("sbuf", [128, 512], "float8_e4m3fn_x4"),
    "hs": ("sbuf", [128, 512], "uint8"),
    "rq": ("sbuf", [128, 512], "float8_e4m3fn_x4"),
    "rs": ("sbuf", [128, 512], "uint8"),
    "yt": ("sbuf", [128, 512], "float32"),
    "pe": ("psum", [128, 2048], "float32"),
    "zp": ("psum", [128, 1536], "float32"),
}
SLICES = ("qx", "mx", "sq", "ro", "ww", "vv", "rc", "nu", "qh", "ic", "ip", "arr", "ym", "cy")
PIECES = ("sc", "tr", "cp")
BLOCKS = ("wq", "ma")
SEMAPHORES = (["%s%d" % (s, c) for s in SLICES for c in range(NS)]
              + ["%s%d%d" % (s, c, b) for s in PIECES for c in range(NS) for b in range(NB)]
              + ["%s%d" % (s, b) for s in BLOCKS for b in range(NB)]
              + ["lx0", "lx1", "lwa", "lwb", "lw2", "one", "idn", "sp", "qw2", "lefta", "leftb", "sent", "sth", "sty"])


def _bits(mask):
    return [i for i in range(mask.bit_length()) if (mask >> i) & 1]


def _plan(T, topo):
    cores = list(T.cores)
    n = len(cores)
    world = range(topo.CORES_PER_HOST * (1 + max(topo.host(c) for c in cores)))
    plan = []
    for s in range(n):
        src, dst = cores[s], cores[(s - 1) % n]
        cand = [c for c in world
                if topo.host(c) == topo.host(src) and topo.chip(c) == topo.chip(src) and c not in cores
                and topo.may_write(src, c) and topo.may_write(c, dst)]
        near = [c for c in cand if topo.die(c) == topo.die(src)] or cand
        far = [c for c in cand if topo.die(c) != topo.die(src)] or cand
        route = []
        for c in range(NS):
            own, other = (near[0], far[-1]), (far[0], near[-1])
            if (NS - 1 - c) % 2:
                own, other = other, own
            if c == 0:
                m = SW // 2
                route.append([(0, 0, m, own[0]), (0, m, SW, other[0]), (1, 0, m, own[1]), (1, m, SW, other[1])])
            else:
                route.append([(0, 0, SW, own[0]), (1, 0, SW, own[1])])
        plan.append((src, dst, route))
    return plan


def _piece(q, s, c, kind, lo, hi):
    if kind == 0:
        return q[:, SW * c + lo:SW * c + hi].bitcast(dt.uint8)
    return s[:, SW * c + lo:SW * c + hi]


def _helper(g, core, T, topo, src, dst, route):
    rid, pid = topo.addr(dst, core)
    out_mask = topo.mask(core, dst)
    landed = len(_bits(topo.mask(src, core)))
    sent = 0
    for c in range(NS):
        for kind, lo, hi, by in route[c]:
            if by != core:
                continue
            g.wait_ge(T.sem["%s%d" % (("ic", "ip")[kind], c)], landed)
            ap = _piece(T.rq, T.rs, c, kind, lo, hi)
            g.remote_dma(out_ap=ap, in_ap=ap, remote_sem=T.sem["arr%d" % c],
                         local_sem=T.sem.sent, pid=pid, routing_id=rid, dma_engine_mask=out_mask)
            sent += len(_bits(out_mask))
    g.wait_ge(T.sem.sent, sent)


def _rank(g, core, T, topo, route, arrivals):
    S = T.sem
    AF, OP = ActivationFunctionType, AluOpType
    ve, te, sc, sy = g.vector, g.tensor, g.scalar, g.sync
    last = NS - 1
    half = NS // 2

    def col(k, c):
        return T.st[:, NS * k + c:NS * k + c + 1]

    def duo(k, c, i, n):
        at = 3 * NS + 2 * NS * k + 2 * c + i
        return T.st[:, at:at + n]

    def sl(t, c, w):
        return t[:, w * c:w * c + w]

    def bank(b):
        return T.pe[:, BANK * b:BANK * b + SW]

    def prod(c):
        return T.zp[:, BANK * (c - 1):BANK * c]

    def prod_b(c, b):
        return bank(b) if c == 0 else T.zp[:, BANK * (c - 1) + SW * b:BANK * (c - 1) + SW * b + SW]

    def turned(c, b):
        return T.rt[:, 4 * SW * c + SW * b:4 * SW * c + SW * b + SW]

    def h_cols(c, b):
        return T.ht[:, 4 * SW * c + b:4 * SW * (c + 1):4]

    hw = 2 * 4 * SW
    sy.dma_start(T.xt[:, 0:4 * SW], T.x[:, 0:4 * SW]).then_inc(S.lx0, 16)
    sc.dma_start(T.w1t[:, 0:hw], T.w1[:, 0:hw]).then_inc(S.lwa, 16)
    sy.dma_start(T.w1t[:, hw:], T.w1[:, hw:]).then_inc(S.lwb, 16)
    sy.dma_start(T.xt[:, 4 * SW:], T.x[:, 4 * SW:]).then_inc(S.lx1, 16)
    sy.dma_start(T.w2t[:], T.w2[:]).then_inc(S.lw2, 16)

    ve.memset(T.ident[:], 1.0).then_inc(S.one, 1)
    g.wait_ge(S.one, 1)
    g.affine_select(T.ident[:], T.ident[:], [[-1, 128]], OP.is_equal, 0.0, 0, 1).then_inc(S.idn, 1)

    def pack_x(c):
        ve.quantize_mx(sl(T.xq, c, SW), sl(T.xs, c, SW), sl(T.xt, c, 4 * SW)).then_inc(S["qx%d" % c], 1)

    def factors(c):
        ve.wait_ge(S["ww%d" % c], 1)
        ve.reciprocal(duo(1, c, 0, 2), duo(0, c, 0, 2)).then_inc(S["rc%d" % c], 1)
        ve.wait_ge(S["vv%d" % c], 1)
        ve.wait_ge(S["rc%d" % c], 1)
        ve.tensor_scalar(col(2, c), duo(1, c, 1, 1), col(1, c), 1.5, OP.mult, OP.add).then_inc(S["nu%d" % c], 1)
        ve.wait_ge(S["nu%d" % c], 1)

    def scale(c):
        for b in range(NB):
            ve.wait_ge(S["ma%d" % b] if c == 0 else S["mx%d" % c], 1)
            ve.tensor_scalar(turned(c, b), prod_b(c, b), duo(1, c, 0, 1), col(2, c), OP.mult, OP.mult).then_inc(S["sc%d%d" % (c, b)], 1)

    def pack_h(c):
        for b in range(NB):
            ve.wait_ge(S["cp%d%d" % (c, b)], 1)
        ve.quantize_mx(sl(T.hq, c, SW), sl(T.hs, c, SW), sl(T.ht, c, 4 * SW)).then_inc(S["qh%d" % c], 1)

    ve.wait_ge(S.lx0, 16)
    pack_x(0)
    for b in range(NB):
        ve.wait_ge(S.lwa if b < NB // 2 else S.lwb, 16)
        ve.quantize_mx(sl(T.w1q, b, SW), sl(T.w1s, b, SW), sl(T.w1t, b, 4 * SW)).then_inc(S["wq%d" % b], 1)
    ve.wait_ge(S.lx1, 16)
    for c in range(1, NS):
        pack_x(c)
    factors(0)
    scale(0)
    factors(1)
    scale(1)
    pack_h(0)
    factors(2)
    scale(2)
    factors(last)
    pack_h(1)
    scale(last)
    pack_h(2)
    ve.wait_ge(S["tr%d%d" % (last, NB - 1)], 1)
    ve.tensor_copy(h_cols(last, NB - 1), bank(NB - 1)).then_inc(S["cp%d%d" % (last, NB - 1)], 1)
    pack_h(last)
    ve.wait_ge(S.lw2, 16)
    ve.quantize_mx(T.w2q[:], T.w2s[:], T.w2t[:]).then_inc(S.qw2, 1)
    for c in range(0, NS, 2):
        ve.wait_ge(S["ym%d" % c], 1)
        ve.tensor_copy(sl(T.yt, c, SW), bank(c)).then_inc(S["cy%d" % c], 1)

    def root(c):
        sc.wait_ge(S["sq%d" % c], 1)
        sc.activation(duo(0, c, 0, 1), col(0, c), AF.Sqrt, bias=EPS, scale=1.0 / ROWS).then_inc(S["ro%d" % c], 1)
        sc.wait_ge(S["ro%d" % c], 1)
        sc.activation(duo(0, c, 1, 1), duo(0, c, 0, 1), AF.Square).then_inc(S["ww%d" % c], 1)
        sc.activation(col(1, c), col(0, c), AF.Identity, bias=-0.5 * EPS, scale=-0.5 / ROWS).then_inc(S["vv%d" % c], 1)

    def stats(c):
        sc.wait_ge(S["mx%d" % c], 1)
        sc.activation(T.sqr[:], prod(c), AF.Square, accum_out=col(0, c)).then_inc(S["sq%d" % c], 1)
        root(c)

    def back(c, blocks):
        for b in blocks:
            sc.wait_ge(S["tr%d%d" % (c, b)], 1)
            sc.activation(h_cols(c, b), bank(b), AF.Copy).then_inc(S["cp%d%d" % (c, b)], 1)

    part = 7 * NS
    for b in range(NB):
        sc.wait_ge(S["ma%d" % b], 1)
        sc.activation(sl(T.sqr, b, SW), bank(b), AF.Square, accum_out=T.st[:, part + b:part + b + 1]).then_inc(S.sp, 1)
    sc.wait_ge(S.sp, NB)
    sc.activation(T.st[:, part + NB:part + 2 * NB], T.st[:, part:part + NB], AF.Copy, accum_out=col(0, 0)).then_inc(S.sq0, 1)
    root(0)
    stats(1)
    stats(2)
    back(0, range(NB))
    stats(last)
    back(1, range(NB))
    back(2, range(NB))
    back(last, range(NB - 1))
    for c in range(1, NS, 2):
        sc.wait_ge(S["ym%d" % c], 1)
        sc.activation(sl(T.yt, c, SW), bank(c), AF.Copy).then_inc(S["cy%d" % c], 1)

    te.wait_ge(S.qx0, 1)
    for b in range(NB):
        te.wait_ge(S["wq%d" % b], 1)
        te.matmul_mx(bank(b), sl(T.xq, 0, SW), sl(T.xs, 0, SW), sl(T.w1q, b, SW), sl(T.w1s, b, SW),
                     True, True).then_inc(S["ma%d" % b], 1)
    for c in range(1, NS):
        te.wait_ge(S["qx%d" % c], 1)
        te.matmul_mx(prod(c), sl(T.xq, c, SW), sl(T.xs, c, SW), T.w1q[:], T.w1s[:], True, True).then_inc(S["mx%d" % c], 1)
    te.wait_ge(S.idn, 1)
    for c in range(NS):
        for b in range(NB):
            te.wait_ge(S["sc%d%d" % (c, b)], 1)
            if c:
                te.wait_ge(S["cp%d%d" % (c - 1, b)], 1)
            te.matmul(bank(b), turned(c, b), T.ident[:], True, True).then_inc(S["tr%d%d" % (c, b)], 1)
    te.wait_ge(S.qw2, 1)
    for c in range(NS):
        te.wait_ge(S["qh%d" % c], 1)
    for c in range(NS):
        te.matmul_mx(bank(c), T.w2q[:, 0:128], T.w2s[:, 0:128], sl(T.hq, c, SW), sl(T.hs, c, SW), True, False)
    for c in range(NS):
        te.wait_ge(S["arr%d" % c], arrivals[c])
        te.matmul_mx(bank(c), T.w2q[:, 128:256], T.w2s[:, 128:256], sl(T.rq, c, SW), sl(T.rs, c, SW),
                     False, True).then_inc(S["ym%d" % c], 1)

    left = [0, 0]
    for c in range(NS):
        g.wait_ge(S["qh%d" % c], 1)
        for kind, lo, hi, to in route[c]:
            rid, pid = topo.addr(to, core)
            engines = topo.mask(core, to)
            g.remote_dma(out_ap=_piece(T.rq, T.rs, c, kind, lo, hi), in_ap=_piece(T.hq, T.hs, c, kind, lo, hi),
                         remote_sem=S["%s%d" % (("ic", "ip")[kind], c)],
                         local_sem=S.lefta if c < half else S.leftb, pid=pid, routing_id=rid, dma_engine_mask=engines)
            left[c // half] += len(_bits(engines))

    hh = 4 * SW * half
    for c in range(half):
        sy.wait_ge(S["qh%d" % c], 1)
    sy.wait_ge(S.lefta, left[0])
    sy.dma_start(T.h[:, 0:hh], T.ht[:, 0:hh]).then_inc(S.sth, 16)
    for c in range(half, NS):
        sy.wait_ge(S["qh%d" % c], 1)
    sy.wait_ge(S.leftb, left[1])
    sy.dma_start(T.h[:, hh:], T.ht[:, hh:]).then_inc(S.sth, 16)
    for c in range(NS):
        sy.wait_ge(S["cy%d" % c], 1)
        sy.dma_start(sl(T.y, c, SW), sl(T.yt, c, SW)).then_inc(S.sty, 16)
    sy.wait_ge(S.sth, 32)
    sy.wait_ge(S.sty, 16 * NS)


def rank_program(g, core, T, topo):
    plan = _plan(T, topo)
    n = len(plan)
    rank = T.rank_of(core)
    if rank is not None:
        src, dst, route = plan[(rank + 1) % n]
        arrivals = [sum(len(_bits(topo.mask(p[3], dst))) for p in route[c]) for c in range(NS)]
        _rank(g, core, T, topo, plan[rank][2], arrivals)
        return
    for src, dst, route in plan:
        if any(p[3] == core for pieces in route for p in pieces):
            _helper(g, core, T, topo, src, dst, route)
